import numpy as np
import ml_dtypes


def mxq(x, axis, fmt="e4m3"):
    dtype, down = {"e4m3": (ml_dtypes.float8_e4m3fn, 7), "e5m2": (ml_dtypes.float8_e5m2, 14)}[fmt]
    v = np.moveaxis(np.asarray(x, np.float32).astype(ml_dtypes.bfloat16).astype(np.float64), axis, -1)
    blocks = v.reshape(v.shape[:-1] + (-1, 32))
    amax = np.abs(blocks).max(-1, keepdims=True)
    byte = np.maximum(np.where(amax > 0, np.frexp(amax)[1] - 1 + 127, 0) - down, 1)
    scale = np.exp2(byte - 127.0)
    codes = (blocks / scale).astype(np.float32).astype(dtype).astype(np.float64)
    return np.moveaxis((codes * scale).reshape(v.shape), -1, axis)


WIDE = False


def mx_kscale(k):
    if not WIDE:
        return np.ones(k)
    levels = np.array([10, -10, 5, -5, 0])
    if k % 512:
        return np.exp2(np.random.permutation(np.resize(levels, k // 32))).repeat(32)
    a = np.empty((k // 512, 16))
    for p in range(k // 512):
        a[p, :8] = np.random.permutation(np.resize(levels, 8))
        for g in range(8):
            far = levels[np.abs(levels - a[p, g]) >= 10]
            a[p, g + 8] = far[np.random.randint(len(far))]
    return np.exp2(a.ravel()).repeat(32)


def f64(x):
    return np.asarray(x).astype(np.float64)


def striped(idx):
    return np.tile(idx.reshape(-1, 16).T, (8, 1)).astype(np.uint16)


def unstriped(offs):
    return offs[:16].T.reshape(-1).astype(np.int64)


E2M1 = np.array([0.0, 0.5, 1.0, 1.5, 2.0, 3.0, 4.0, 6.0, -0.0, -0.5, -1.0, -1.5, -2.0, -3.0, -4.0, -6.0])


def pack_weight(w, fmt):
    k, n = w.shape
    w = f64(np.asarray(w, np.float32).astype(ml_dtypes.bfloat16)).reshape(k // 32, 32, n)
    amax = np.abs(w).max(1)
    if fmt == "e4m3":
        byte = np.frexp(amax)[1] - 1 + 127 - 7
    else:
        mant, ex = np.frexp(amax / 6.0)
        byte = np.where(mant > 0.5, ex, ex - 1) + 127
    byte = np.clip(np.where(amax > 0, byte, 1), 1, 254)
    scaled = (w * np.exp2(127.0 - byte)[:, None, :]).reshape(k, n).astype(np.float32)
    by_word = np.ascontiguousarray(scaled.reshape(k // 512, 128, 4, n).transpose(0, 1, 3, 2))
    if fmt == "e4m3":
        words = by_word.astype(ml_dtypes.float8_e4m3fn).view(np.uint8)
    else:
        c = by_word.astype(ml_dtypes.float4_e2m1fn).view(np.uint8) & 0xF
        words = (c[..., 0::2] | (c[..., 1::2] << 4)).reshape(k // 512, 128, 2 * n)
    return np.ascontiguousarray(words), np.ascontiguousarray(byte.astype(np.uint8).reshape(k // 512, 16, n))


def unpack_weight(words, scales, fmt):
    g, _, n = scales.shape
    words = np.ascontiguousarray(words).reshape(g, 128, n, -1)
    if fmt == "e4m3":
        vals = words.view(ml_dtypes.float8_e4m3fn).astype(np.float64)
    else:
        nib = np.empty((g, 128, n, 4), np.uint8)
        nib[..., 0::2] = words & 0xF
        nib[..., 1::2] = words >> 4
        vals = E2M1[nib]
    vals = vals * np.repeat(np.exp2(scales.astype(np.float64) - 127.0), 8, axis=1)[..., None]
    return vals.transpose(0, 1, 3, 2).reshape(g * 512, n)


def gelu(v):
    return 0.5 * v * (1.0 + np.tanh(np.sqrt(2.0 / np.pi) * (v + 0.044715 * v**3)))


def often(T, S):
    return np.random.permutation(T)[(T * np.random.uniform(0, 1, S) ** 4).astype(np.int64)]


def bf(x):
    return np.asarray(x, np.float32).astype(ml_dtypes.bfloat16)


def planes(Y):
    n, m = Y.shape
    b = f64(bf(Y)).reshape(n // 32, 32, m)
    amax = np.abs(b).max(1)
    byte = np.clip(np.where(amax > 0, np.frexp(amax)[1] - 1 + 127 - 7, 1), 1, 254)
    codes = (b * np.exp2(127.0 - byte)[:, None, :]).reshape(n, m).astype(np.float32).astype(ml_dtypes.float8_e4m3fn).view(np.uint8)
    words = codes.reshape(n // 512, 128, 4, m).transpose(0, 1, 3, 2)
    return np.ascontiguousarray(words), np.ascontiguousarray(byte.astype(np.uint8).reshape(n // 512, 16, m))


K, K2, T, S, P, H, N = 1024, 512, 4096, 1024, 512, 1024, 512

def setup_inputs():
    n = np.random.standard_normal
    s, s2, u = mx_kscale(K)[:, None], mx_kscale(K2)[:, None], mx_kscale(H)[:, None]
    d = {}
    d["tab_words"], d["tab_scales"] = pack_weight(n((K, T)) * s, "e4m3")
    d["tab2_words"], d["tab2_scales"] = pack_weight(n((K2, T)) * s2, "e4m3")
    d["tab3_words"], d["tab3_scales"] = pack_weight(n((K2, T)) * s2, "e4m3")
    d["offs"] = striped(np.random.permutation(T)[:S])
    d["offs2"] = striped(np.random.permutation(T)[:S])
    d["offs3"] = striped(np.random.permutation(T)[:S])
    d["pos1"] = striped(np.random.permutation(S)[:P])
    d["pos2"] = striped(often(S, P))
    d["pos3"] = striped(often(S, P))
    d["wa"] = (n((K, H)) / K**0.5 / s * u.T).astype(np.float32)
    d["wb_words"], d["wb_scales"] = pack_weight(n((K2, H)) / K2**0.5 / s2 * u.T, "e2m1")
    d["wd_words"], d["wd_scales"] = pack_weight(n((K2, H)) / K2**0.5 / s2 * u.T, "e4m3")
    d["wo"] = (0.6 * n((H, N)) / H**0.5 / u * np.exp(0.8 * n(N))).astype(np.float32)
    return d

def reference(tab_words, tab_scales, tab2_words, tab2_scales, tab3_words, tab3_scales, offs, offs2, offs3, pos1, pos2, pos3, wa, wb_words, wb_scales, wd_words, wd_scales, wo):
    v = unpack_weight(tab_words, tab_scales, "e4m3")[:, unstriped(offs)]
    v2 = unpack_weight(tab2_words, tab2_scales, "e4m3")[:, unstriped(offs2)]
    v3 = unpack_weight(tab3_words, tab3_scales, "e4m3")[:, unstriped(offs3)]
    a = mxq(f64(wa), 0, "e4m3").T @ v
    b = unpack_weight(wb_words, wb_scales, "e2m1").T @ v2
    d = unpack_weight(wd_words, wd_scales, "e4m3").T @ v3
    both = np.square(a[:, unstriped(pos1)]) + np.square(b[:, unstriped(pos2)])
    z = np.sqrt(both) - d[:, unstriped(pos3)]
    y = mxq(f64(wo), 0, "e4m3").T @ mxq(z, 0, "e4m3")
    words, scales = planes(y)
    return y, words, scales

@@ -1,0 +1,276 @@
+from contextlib import ExitStack
+
+import concourse.mybir as mybir
+
+K, K2, T, S, P2, H, N = 1024, 512, 4096, 1024, 512, 1024, 512
+FLOPS = 2 * H * S * (K + 2 * K2) + 2 * N * P2 * H
+
+F32 = mybir.dt.float32
+BF16 = mybir.dt.bfloat16
+I32 = mybir.dt.int32
+U32 = mybir.dt.uint32
+U16 = mybir.dt.uint16
+U8 = mybir.dt.uint8
+FP8X4 = mybir.dt.float8_e4m3fn_x4
+FP4X4 = mybir.dt.float4_e2m1fn_x4
+ACT = mybir.ActivationFunctionType
+ALU = mybir.AluOpType
+
+P = 128
+BANK = 512
+HALF = 256
+
+
+def tile_list_drum_assay_features_kernel(
+    tc, tab_words, tab_scales, tab2_words, tab2_scales, tab3_words, tab3_scales,
+    offs, offs2, offs3, pos1, pos2, pos3, wa, wb_words, wb_scales, wd_words, wd_scales, wo,
+    out_0, out_1, out_2,
+):
+    nc = tc.nc
+    with ExitStack() as ctx:
+        lists = ctx.enter_context(tc.tile_pool(name="lists", bufs=1))
+        keep = ctx.enter_context(tc.tile_pool(name="keep", bufs=1))
+        rings = ctx.enter_context(tc.tile_pool(name="rings", bufs=1))
+        arena = ctx.enter_context(tc.tile_pool(name="arena", bufs=1))
+        psum = ctx.enter_context(tc.psum_pool(name="psum", bufs=1))
+
+        def held(shape, dtype, name):
+            return keep.tile(shape, dtype, name=name, align_bytes=64)
+
+        def placed(shape, dtype, name, kib):
+            return arena.tile(shape, dtype, name=name, offset=int(1024 * kib), align_bytes=64)
+
+        def small(shape, dtype, name):
+            return rings.tile(shape, dtype, name=name, tag="small", bufs=4, align_bytes=64)
+
+        def load_list(src, name):
+            tile = lists.tile(list(src.shape), U16, name=name)
+            nc.sync.dma_start(tile[:], src)
+            return tile
+
+        def load_words(src, name, kib):
+            tile = placed([P, T], I32, name, kib)
+            nc.sync.dma_start(tile[:], src.rearrange("p n t -> p (n t)").bitcast(I32))
+            return tile
+
+        def load_scales(tile, src, zeroed_by, queues):
+            passes = src.shape[0]
+            zeroed_by.memset(tile[:].bitcast(I32), 0)
+            for q, queue in enumerate(queues):
+                rows = src[0, 4 * q : 4 * q + 4, :] if passes == 1 else src[:, 4 * q : 4 * q + 4, :]
+                queue.dma_start(tile[32 * q : 32 * q + 4 * passes, :].bitcast(I32), rows.bitcast(I32))
+            return tile
+
+        def gather_words(window, offsets, halves):
+            for h, picked in enumerate(halves):
+                nc.vector.tensor_copy(picked[:], window[:].bitcast(U32).indirect(offsets[:, 32 * h : 32 * h + 32]))
+            return halves
+
+        def gather_scales(window, offsets, picked):
+            nc.vector.tensor_copy(picked[:], window[:].indirect(offsets[:]))
+            return picked
+
+        def deal(raw, name):
+            dealt = held(list(raw.shape), U8, name)
+            nc.vector.tensor_copy(
+                dealt[:].bitcast(I32).rearrange("p (t g i) -> p g t i", t=4, g=32),
+                raw[:].bitcast(I32).rearrange("p (g t i) -> p g t i", t=4, g=32),
+            )
+            return dealt
+
+        def quantise(rounded, name):
+            width = rounded.shape[1] // 4
+            codes = held([P, width], U32, name + "_codes")
+            scales = held([P, width], U8, name + "_scales")
+            nc.vector.quantize_mx(codes[:].bitcast(FP8X4), scales[:], rounded[:])
+            return codes, scales
+
+        offs2_t = load_list(offs2, "offs2_t")
+        wb_raw = placed([P, 2 * H], U8, "wb_raw", 61)
+        nc.sync.dma_start(wb_raw[:].bitcast(I32), wb_words[0].bitcast(I32))
+        offs3_t = load_list(offs3, "offs3_t")
+        offs_t = load_list(offs, "offs_t")
+        pos2_t = load_list(pos2, "pos2_t")
+        pos1_t = load_list(pos1, "pos1_t")
+        pos3_t = load_list(pos3, "pos3_t")
+        tab2_win = load_words(tab2_words[0], "tab2_win", 20)
+        tab2_scale_win = load_scales(placed([P, T], U8, "tab2_scale_win", 13), tab2_scales, nc.vector, [nc.scalar] * 4)
+        wb_scale_raw = load_scales(placed([P, H], U8, "wb_scale_raw", 17.5), wb_scales, nc.vector, [nc.scalar] * 2 + [nc.gpsimd] * 2)
+        tab3_scale_win = load_scales(placed([P, T], U8, "tab3_scale_win", 37), tab3_scales, nc.vector, [nc.scalar] * 4)
+        wd_scale_raw = load_scales(placed([P, H], U8, "wd_scale_raw", 53), wd_scales, nc.vector, [nc.gpsimd] * 4)
+
+        wb_dealt = deal(wb_raw, "wb_dealt")
+        v2_scales = gather_scales(tab2_scale_win, offs2_t, held([P, S], U8, "v2_scales"))
+        wb_scale_dealt = deal(wb_scale_raw, "wb_scale_dealt")
+        v2_words = gather_words(tab2_win, offs2_t, [placed([P, BANK], U32, "v2_words%d" % h, 18 - 2 * h) for h in range(2)])
+
+        wd_raw = placed([P, 4 * H], U8, "wd_raw", 61)
+        nc.sync.dma_start(wd_raw[:].bitcast(I32), wd_words[0].rearrange("p n t -> p (n t)").bitcast(I32))
+        tab3_win = load_words(tab3_words[0], "tab3_win", 0)
+        v3_scales = gather_scales(tab3_scale_win, offs3_t, placed([P, S], U8, "v3_scales", 20))
+        wd_dealt = deal(wd_raw, "wd_dealt")
+        wd_scale_dealt = deal(wd_scale_raw, "wd_scale_dealt")
+        v3_words = gather_words(tab3_win, offs3_t, [held([P, BANK], U32, "v3_words%d" % h) for h in range(2)])
+
+        tab_win = [load_words(tab_words[a], "tab_win%d" % a, 21 + 16 * a) for a in range(2)]
+        tab_scale_win = load_scales(placed([P, T], U8, "tab_scale_win", 61), tab_scales, nc.gpsimd, [nc.sync] * 4)
+        v_scales = gather_scales(tab_scale_win, offs_t, held([P, S], U8, "v_scales"))
+        v_words = [
+            gather_words(tab_win[a], offs_t, [held([P, BANK], U32, "v_words%d%d" % (a, h)) for h in range(2)])
+            for a in range(2)
+        ]
+
+        wa_at = {(0, 0): 0, (0, 1): 53, (1, 0): 21, (1, 1): 29}
+        wa_raw = {}
+        for (b, a), kib in wa_at.items():
+            wa_raw[b, a] = placed([P, 4, BANK], F32, "wa_raw%d%d" % (b, a), kib)
+            rows = wa[BANK * a : BANK * (a + 1), BANK * b : BANK * (b + 1)]
+            nc.sync.dma_start(wa_raw[b, a][:], rows.rearrange("(p j) c -> p j c", j=4))
+
+        def first_stage(slices, passes, func, tag):
+            windows = {}
+            for pair in (slices[i : i + 2] for i in range(0, len(slices), 2)):
+                for s in pair:
+                    windows[s] = rings.tile([P, S], F32, name="%s%d%d" % (tag, s[0], s[1]), tag=tag, bufs=8)
+                for h in range(2):
+                    cols = slice(BANK * h, BANK * (h + 1))
+                    for s in pair:
+                        acc = psum.tile([P, BANK], F32, name="acc", tag="acc", bufs=4)
+                        operands = passes(s, h, cols)
+                        for n, (w, w_scale, v, v_scale) in enumerate(operands):
+                            nc.tensor.matmul_mx(
+                                acc[:], lhsT=w, lhsT_scale=w_scale, rhs=v, rhs_scale=v_scale,
+                                start=n == 0, stop=n == len(operands) - 1,
+                            )
+                        nc.scalar.activation(windows[s][:, cols], acc[:], func)
+            return windows
+
+        all_slices = [(b, t) for b in range(2) for t in range(4)]
+
+        def b_passes(s, h, cols):
+            c = HALF * s[1] + P * s[0]
+            return [(wb_dealt[:, 2 * c : 2 * c + 2 * P].bitcast(FP4X4), wb_scale_dealt[:, c : c + P],
+                     v2_words[h][:].bitcast(FP8X4), v2_scales[:, cols])]
+
+        def d_passes(s, h, cols):
+            c = HALF * s[1] + P * s[0]
+            return [(wd_dealt[:, 4 * c : 4 * c + 4 * P].bitcast(FP8X4), wd_scale_dealt[:, c : c + P],
+                     v3_words[h][:].bitcast(FP8X4), v3_scales[:, cols])]
+
+        b_sq = first_stage(all_slices, b_passes, ACT.Square, "sq")
+        d_win = first_stage(all_slices, d_passes, ACT.Copy, "d")
+        b_picked = {}
+
+        def pick_b(slices, kib):
+            for n, s in enumerate(slices):
+                b_picked[s] = placed([P, P2], F32, "b_picked%d%d" % s, kib + 2 * n)
+                nc.vector.tensor_copy(b_picked[s][:], b_sq[s][:].indirect(pos2_t[:]))
+
+        wa_q = {}
+
+        def quantise_wa(b, a, copy):
+            name = "wa%d%d" % (b, a)
+            rounded = small([P, 4 * BANK], BF16, name + "_bf16")
+            copy(
+                rounded[:].rearrange("p (t g i j) -> p g t i j", t=4, i=8, j=4),
+                wa_raw[b, a][:].rearrange("p j (g t i) -> p g t i j", t=4, i=8),
+            )
+            wa_q[b, a] = quantise(rounded, name)
+
+        def a_passes(s, h, cols):
+            c = slice(P * s[1], P * (s[1] + 1))
+            return [(wa_q[s[0], a][0][:, c].bitcast(FP8X4), wa_q[s[0], a][1][:, c],
+                     v_words[a][h][:].bitcast(FP8X4), v_scales[4 * a : P, cols]) for a in range(2)]
+
+        def root(s, a_sq, total):
+            nc.vector.tensor_tensor(total, a_sq[s][:].indirect(pos1_t[:]), b_picked[s][:], ALU.add)
+            nc.scalar.activation(b_picked[s][:], total, ACT.Sqrt)
+
+        def subtract(s, first, count, neg_z):
+            picked_d = d_win[s][:].indirect(pos3_t[:, first // 16 : (first + count) // 16])
+            nc.vector.tensor_tensor(neg_z, picked_d, b_picked[s][:, first : first + count], ALU.subtract)
+
+        def quantise_z(neg_z, name):
+            rounded = small([P, 4 * neg_z.shape[2]], BF16, name + "_bf16")
+            nc.vector.tensor_scalar(
+                rounded[:].rearrange("p (c i t) -> p c t i", t=4, i=4),
+                neg_z[:].rearrange("p t (c i) -> p c t i", i=4),
+                -1.0, None, ALU.mult,
+            )
+            return quantise(rounded, name)
+
+        pick_b(all_slices[0:4], 8)
+        pick_b(all_slices[4:6], 37)
+        quantise_wa(0, 0, nc.vector.tensor_copy)
+        quantise_wa(0, 1, nc.scalar.copy)
+        pick_b(all_slices[6:8], 53)
+        quantise_wa(1, 0, nc.scalar.copy)
+        wo_raw = [placed([P, 4, N], F32, "wo_raw%d" % b, kib) for b, kib in enumerate((0, 45))]
+        for b in range(2):
+            rows = wo[BANK * b : BANK * (b + 1), :].rearrange("(g j i) n -> j g i n", j=4, i=8)
+            for j in range(4):
+                nc.sync.dma_start(wo_raw[b][:, j, :], rows[j])
+
+        a_sq0 = first_stage(all_slices[0:4], a_passes, ACT.Square, "sq")
+        neg_z0 = placed([P, 4, P2], F32, "neg_z0", 65)
+        for t in range(4):
+            if t == 2:
+                quantise_wa(1, 1, nc.scalar.copy)
+            root((0, t), a_sq0, neg_z0[:, t, :])
+            subtract((0, t), 0, P2, neg_z0[:, t, :])
+        z0 = quantise_z(neg_z0, "z0")
+
+        a_sq1 = first_stage(all_slices[4:8], a_passes, ACT.Square, "sq")
+        total1 = placed([P, 4, P2], F32, "total1", 21)
+        for t in range(4):
+            root((1, t), a_sq1, total1[:, t, :])
+        wo_q = []
+        for b in range(2):
+            rounded = placed([P, 4 * N], BF16, "wo%d_bf16" % b, 65 + 4 * b)
+            nc.scalar.copy(
+                rounded[:].rearrange("p (t q j) -> p q j t", t=4, j=4),
+                wo_raw[b][:].rearrange("p j (q t) -> p q j t", t=4),
+            )
+            wo_q.append(quantise(rounded, "wo%d" % b))
+
+        y_scales = held([P, P2], U8, "y_scales")
+        y_rows = out_0.rearrange("(p t) m -> p t m", t=4)
+        y_words = out_1[0].rearrange("p m t -> p (m t)").bitcast(I32)
+
+        def project(acc, t, b, z, cols):
+            c = slice(P * t, P * (t + 1))
+            nc.tensor.matmul_mx(
+                acc[:], lhsT=wo_q[b][0][:, c].bitcast(FP8X4), lhsT_scale=wo_q[b][1][:, c],
+                rhs=z[0][:, cols].bitcast(FP8X4), rhs_scale=z[1][:, cols], start=b == 0, stop=b == 1,
+            )
+
+        for h in range(2):
+            last = h == 1
+            cols = slice(HALF * h, HALF * (h + 1))
+            accs = [psum.tile([P, HALF], F32, name="y_acc", tag="tail" if last else "acc", bufs=4) for t in range(4)]
+            neg_z1 = placed([P, 4, HALF], F32, "neg_z1_%d" % h, 29 + 4 * h)
+            for t in range(4):
+                subtract((1, t), HALF * h, HALF, neg_z1[:, t, :])
+            z1 = quantise_z(neg_z1, "z1_%d" % h)
+            y = placed([P, 4, HALF], F32, "y%d" % h, 8 + 4 * h)
+            for t in range(4):
+                project(accs[t], t, 0, z0, cols)
+                project(accs[t], t, 1, z1, slice(0, HALF))
+                if last and t % 2 == 1:
+                    nc.vector.tensor_copy(y[:, t, :], accs[t][:])
+                else:
+                    nc.scalar.copy(y[:, t, :], accs[t][:])
+            nc.sync.dma_start(y_rows[:, :, cols], y[:])
+            rounded = small([P, 4 * HALF], BF16, "y%d_bf16" % h)
+            dst = rounded[:].rearrange("p (c i t) -> p c t i", t=4, i=4)
+            src = y[:].rearrange("p t (c i) -> p c t i", i=4)
+            if last:
+                nc.vector.tensor_copy(dst, src)
+            else:
+                nc.scalar.copy(dst, src)
+            y_codes = held([P, HALF], I32, "y_codes%d" % h)
+            nc.vector.quantize_mx(y_codes[:].bitcast(FP8X4), y_scales[:, cols], rounded[:])
+            nc.sync.dma_start(y_words[:, cols], y_codes[:])
+        for q in range(4):
+            queue = nc.scalar if q % 2 else nc.sync
+            queue.dma_start(out_2[0, 4 * q : 4 * q + 4, :].bitcast(I32), y_scales[32 * q : 32 * q + 4, :].bitcast(I32))

@@ -53,25 +53,26 @@ def tile_list_drum_assay_features_kernel(
             nc.sync.dma_start(tile[:], src.rearrange("p n t -> p (n t)").bitcast(I32))
             return tile
 
-        def load_scales(tile, src, zeroed_by, queues):
+        def load_scales(tile, src, queue):
             passes = src.shape[0]
-            zeroed_by.memset(tile[:].bitcast(I32), 0)
-            for q, queue in enumerate(queues):
+            for q in range(4):
                 rows = src[0, 4 * q : 4 * q + 4, :] if passes == 1 else src[:, 4 * q : 4 * q + 4, :]
                 queue.dma_start(tile[32 * q : 32 * q + 4 * passes, :].bitcast(I32), rows.bitcast(I32))
             return tile
 
-        def gather_words(window, offsets, halves):
-            for h, picked in enumerate(halves):
-                nc.vector.tensor_copy(picked[:], window[:].bitcast(U32).indirect(offsets[:, 32 * h : 32 * h + 32]))
-            return halves
+        def zeroed(tile, engine):
+            engine.memset(tile[:].bitcast(I32), 0)
+            return tile
+
+        def gather_words(window, offsets, picked):
+            nc.vector.tensor_copy(picked[:], window[:].bitcast(U32).indirect(offsets[:]))
+            return picked
 
         def gather_scales(window, offsets, picked):
             nc.vector.tensor_copy(picked[:], window[:].indirect(offsets[:]))
             return picked
 
-        def deal(raw, name):
-            dealt = held(list(raw.shape), U8, name)
+        def deal(raw, dealt):
             nc.vector.tensor_copy(
                 dealt[:].bitcast(I32).rearrange("p (t g i) -> p g t i", t=4, g=32),
                 raw[:].bitcast(I32).rearrange("p (g t i) -> p g t i", t=4, g=32),
@@ -86,41 +87,44 @@ def tile_list_drum_assay_features_kernel(
             return codes, scales
 
         offs2_t = load_list(offs2, "offs2_t")
-        wb_raw = placed([P, 2 * H], U8, "wb_raw", 61)
+        tab2_win = load_words(tab2_words[0], "tab2_win", 34)
+        wb_raw = held([P, 2 * H], U8, "wb_raw")
         nc.sync.dma_start(wb_raw[:].bitcast(I32), wb_words[0].bitcast(I32))
         offs3_t = load_list(offs3, "offs3_t")
         offs_t = load_list(offs, "offs_t")
         pos2_t = load_list(pos2, "pos2_t")
         pos1_t = load_list(pos1, "pos1_t")
         pos3_t = load_list(pos3, "pos3_t")
-        tab2_win = load_words(tab2_words[0], "tab2_win", 20)
-        tab2_scale_win = load_scales(placed([P, T], U8, "tab2_scale_win", 13), tab2_scales, nc.vector, [nc.scalar] * 4)
-        wb_scale_raw = load_scales(placed([P, H], U8, "wb_scale_raw", 17.5), wb_scales, nc.vector, [nc.scalar] * 2 + [nc.gpsimd] * 2)
-        tab3_scale_win = load_scales(placed([P, T], U8, "tab3_scale_win", 37), tab3_scales, nc.vector, [nc.scalar] * 4)
-        wd_scale_raw = load_scales(placed([P, H], U8, "wd_scale_raw", 53), wd_scales, nc.vector, [nc.gpsimd] * 4)
+        tab2_scale_win = load_scales(zeroed(placed([P, T], U8, "tab2_scale_win", 72), nc.gpsimd), tab2_scales, nc.gpsimd)
+        wb_scale_raw = load_scales(zeroed(placed([P, H], U8, "wb_scale_raw", 76), nc.vector), wb_scales, nc.sync)
+        tab3_scale_win = load_scales(zeroed(placed([P, T], U8, "tab3_scale_win", 67), nc.vector), tab3_scales, nc.sync)
+        wd_scale_raw = load_scales(zeroed(held([P, H], U8, "wd_scale_raw"), nc.vector), wd_scales, nc.sync)
+        warm = placed([P, 32], F32, "warm", 10 - 1 / 16)
+        nc.vector.memset(warm[:], 1.0)
+        nc.scalar.activation(warm[:], warm[:], ACT.Sqrt)
 
-        wb_dealt = deal(wb_raw, "wb_dealt")
-        v2_scales = gather_scales(tab2_scale_win, offs2_t, held([P, S], U8, "v2_scales"))
-        wb_scale_dealt = deal(wb_scale_raw, "wb_scale_dealt")
-        v2_words = gather_words(tab2_win, offs2_t, [placed([P, BANK], U32, "v2_words%d" % h, 18 - 2 * h) for h in range(2)])
-
-        wd_raw = placed([P, 4 * H], U8, "wd_raw", 61)
-        nc.sync.dma_start(wd_raw[:].bitcast(I32), wd_words[0].rearrange("p n t -> p (n t)").bitcast(I32))
-        tab3_win = load_words(tab3_words[0], "tab3_win", 0)
-        v3_scales = gather_scales(tab3_scale_win, offs3_t, placed([P, S], U8, "v3_scales", 20))
-        wd_dealt = deal(wd_raw, "wd_dealt")
-        wd_scale_dealt = deal(wd_scale_raw, "wd_scale_dealt")
-        v3_words = gather_words(tab3_win, offs3_t, [held([P, BANK], U32, "v3_words%d" % h) for h in range(2)])
-
-        tab_win = [load_words(tab_words[a], "tab_win%d" % a, 21 + 16 * a) for a in range(2)]
-        tab_scale_win = load_scales(placed([P, T], U8, "tab_scale_win", 61), tab_scales, nc.gpsimd, [nc.sync] * 4)
-        v_scales = gather_scales(tab_scale_win, offs_t, held([P, S], U8, "v_scales"))
-        v_words = [
-            gather_words(tab_win[a], offs_t, [held([P, BANK], U32, "v_words%d%d" % (a, h)) for h in range(2)])
-            for a in range(2)
+        v2_words = gather_words(tab2_win, offs2_t, held([P, S], U32, "v2_words"))
+        wb_dealt = deal(wb_raw, held([P, 2 * H], U8, "wb_dealt"))
+        wb_scale_dealt = deal(wb_scale_raw, held([P, H], U8, "wb_scale_dealt"))
+        v2_scales = [
+            gather_scales(tab2_scale_win, offs2_t[:, 32 * h : 32 * h + 32], held([P, BANK], U8, "v2_scales%d" % h))
+            for h in range(2)
         ]
 
-        wa_at = {(0, 0): 0, (0, 1): 53, (1, 0): 21, (1, 1): 29}
+        tab3_win = load_words(tab3_words[0], "tab3_win", 10)
+        wd_raw = placed([P, 4 * H], U8, "wd_raw", 6)
+        nc.sync.dma_start(wd_raw[:].bitcast(I32), wd_words[0].rearrange("p n t -> p (n t)").bitcast(I32))
+        v3_scales = gather_scales(tab3_scale_win, offs3_t, placed([P, S], U8, "v3_scales", 75.5))
+        v3_words = gather_words(tab3_win, offs3_t, placed([P, S], U32, "v3_words", 68))
+        wd_dealt = deal(wd_raw, placed([P, 4 * H], U8, "wd_dealt", 19))
+        wd_scale_dealt = deal(wd_scale_raw, placed([P, H], U8, "wd_scale_dealt", 18))
+
+        tab_win = [load_words(tab_words[a], "tab_win%d" % a, 36 + 16 * a) for a in range(2)]
+        tab_scale_win = load_scales(zeroed(placed([P, T], U8, "tab_scale_win", 31), nc.gpsimd), tab_scales, nc.sync)
+        v_scales = gather_scales(tab_scale_win, offs_t, held([P, S], U8, "v_scales"))
+        v_words = [gather_words(tab_win[a], offs_t, held([P, S], U32, "v_words%d" % a)) for a in range(2)]
+
+        wa_at = {(0, 0): 23, (0, 1): 10, (1, 0): 36, (1, 1): 44}
         wa_raw = {}
         for (b, a), kib in wa_at.items():
             wa_raw[b, a] = placed([P, 4, BANK], F32, "wa_raw%d%d" % (b, a), kib)
@@ -150,21 +154,22 @@ def tile_list_drum_assay_features_kernel(
         def b_passes(s, h, cols):
             c = HALF * s[1] + P * s[0]
             return [(wb_dealt[:, 2 * c : 2 * c + 2 * P].bitcast(FP4X4), wb_scale_dealt[:, c : c + P],
-                     v2_words[h][:].bitcast(FP8X4), v2_scales[:, cols])]
+                     v2_words[:, cols].bitcast(FP8X4), v2_scales[h][:])]
 
         def d_passes(s, h, cols):
             c = HALF * s[1] + P * s[0]
             return [(wd_dealt[:, 4 * c : 4 * c + 4 * P].bitcast(FP8X4), wd_scale_dealt[:, c : c + P],
-                     v3_words[h][:].bitcast(FP8X4), v3_scales[:, cols])]
+                     v3_words[:, cols].bitcast(FP8X4), v3_scales[:, cols])]
 
         b_sq = first_stage(all_slices, b_passes, ACT.Square, "sq")
         d_win = first_stage(all_slices, d_passes, ACT.Copy, "d")
         b_picked = {}
 
         def pick_b(slices, kib):
+            picked = placed([P, len(slices), P2], F32, "b_picked%d%d" % slices[0], kib)
             for n, s in enumerate(slices):
-                b_picked[s] = placed([P, P2], F32, "b_picked%d%d" % s, kib + 2 * n)
-                nc.vector.tensor_copy(b_picked[s][:], b_sq[s][:].indirect(pos2_t[:]))
+                b_picked[s] = picked[:, n, :]
+                nc.vector.tensor_copy(b_picked[s], b_sq[s][:].indirect(pos2_t[:]))
 
         wa_q = {}
 
@@ -180,53 +185,54 @@ def tile_list_drum_assay_features_kernel(
         def a_passes(s, h, cols):
             c = slice(P * s[1], P * (s[1] + 1))
             return [(wa_q[s[0], a][0][:, c].bitcast(FP8X4), wa_q[s[0], a][1][:, c],
-                     v_words[a][h][:].bitcast(FP8X4), v_scales[4 * a : P, cols]) for a in range(2)]
+                     v_words[a][:, cols].bitcast(FP8X4), v_scales[4 * a : P, cols]) for a in range(2)]
 
         def root(s, a_sq, total):
-            nc.vector.tensor_tensor(total, a_sq[s][:].indirect(pos1_t[:]), b_picked[s][:], ALU.add)
-            nc.scalar.activation(b_picked[s][:], total, ACT.Sqrt)
+            nc.vector.tensor_tensor(total, a_sq[s][:].indirect(pos1_t[:]), b_picked[s], ALU.add)
+            nc.scalar.activation(b_picked[s], total, ACT.Sqrt)
 
         def subtract(s, first, count, neg_z):
             picked_d = d_win[s][:].indirect(pos3_t[:, first // 16 : (first + count) // 16])
             nc.vector.tensor_tensor(neg_z, picked_d, b_picked[s][:, first : first + count], ALU.subtract)
 
-        def quantise_z(neg_z, name):
+        def quantise_z(neg_z, name, on_vector):
             rounded = small([P, 4 * neg_z.shape[2]], BF16, name + "_bf16")
-            nc.vector.tensor_scalar(
-                rounded[:].rearrange("p (c i t) -> p c t i", t=4, i=4),
-                neg_z[:].rearrange("p t (c i) -> p c t i", i=4),
-                -1.0, None, ALU.mult,
-            )
+            dst = rounded[:].rearrange("p (c i t) -> p c t i", t=4, i=4)
+            src = neg_z[:].rearrange("p t (c i) -> p c t i", i=4)
+            if on_vector:
+                nc.vector.tensor_scalar(dst, src, -1.0, None, ALU.mult)
+            else:
+                nc.scalar.activation(dst, src, ACT.Copy, scale=-1.0)
             return quantise(rounded, name)
 
-        pick_b(all_slices[0:4], 8)
-        pick_b(all_slices[4:6], 37)
-        quantise_wa(0, 0, nc.vector.tensor_copy)
+        pick_b(all_slices[0:4], 2)
+        pick_b(all_slices[4:6], 52)
+        quantise_wa(0, 0, nc.scalar.copy)
         quantise_wa(0, 1, nc.scalar.copy)
-        pick_b(all_slices[6:8], 53)
+        pick_b(all_slices[6:8], 10)
         quantise_wa(1, 0, nc.scalar.copy)
-        wo_raw = [placed([P, 4, N], F32, "wo_raw%d" % b, kib) for b, kib in enumerate((0, 45))]
+        wo_raw = [placed([P, 4, N], F32, "wo_raw%d" % b, kib) for b, kib in enumerate((23, 60))]
         for b in range(2):
             rows = wo[BANK * b : BANK * (b + 1), :].rearrange("(g j i) n -> j g i n", j=4, i=8)
             for j in range(4):
                 nc.sync.dma_start(wo_raw[b][:, j, :], rows[j])
 
         a_sq0 = first_stage(all_slices[0:4], a_passes, ACT.Square, "sq")
-        neg_z0 = placed([P, 4, P2], F32, "neg_z0", 65)
+        neg_z0 = placed([P, 4, P2], F32, "neg_z0", 78)
         for t in range(4):
-            if t == 2:
+            if t == 1:
                 quantise_wa(1, 1, nc.scalar.copy)
             root((0, t), a_sq0, neg_z0[:, t, :])
             subtract((0, t), 0, P2, neg_z0[:, t, :])
-        z0 = quantise_z(neg_z0, "z0")
+        z0 = quantise_z(neg_z0, "z0", True)
 
         a_sq1 = first_stage(all_slices[4:8], a_passes, ACT.Square, "sq")
-        total1 = placed([P, 4, P2], F32, "total1", 21)
+        total1 = placed([P, 4, P2], F32, "total1", 36)
         for t in range(4):
             root((1, t), a_sq1, total1[:, t, :])
         wo_q = []
         for b in range(2):
-            rounded = placed([P, 4 * N], BF16, "wo%d_bf16" % b, 65 + 4 * b)
+            rounded = placed([P, 4 * N], BF16, "wo%d_bf16" % b, 78 + 4 * b)
             nc.scalar.copy(
                 rounded[:].rearrange("p (t q j) -> p q j t", t=4, j=4),
                 wo_raw[b][:].rearrange("p j (q t) -> p q j t", t=4),
@@ -248,11 +254,11 @@ def tile_list_drum_assay_features_kernel(
             last = h == 1
             cols = slice(HALF * h, HALF * (h + 1))
             accs = [psum.tile([P, HALF], F32, name="y_acc", tag="tail" if last else "acc", bufs=4) for t in range(4)]
-            neg_z1 = placed([P, 4, HALF], F32, "neg_z1_%d" % h, 29 + 4 * h)
+            neg_z1 = placed([P, 4, HALF], F32, "neg_z1_%d" % h, 44 + 4 * h)
             for t in range(4):
                 subtract((1, t), HALF * h, HALF, neg_z1[:, t, :])
-            z1 = quantise_z(neg_z1, "z1_%d" % h)
-            y = placed([P, 4, HALF], F32, "y%d" % h, 8 + 4 * h)
+            z1 = quantise_z(neg_z1, "z1_%d" % h, last)
+            y = placed([P, 4, HALF], F32, "y%d" % h, 2 + 4 * h)
             for t in range(4):
                 project(accs[t], t, 0, z0, cols)
                 project(accs[t], t, 1, z1, slice(0, HALF))
@@ -270,7 +276,7 @@ def tile_list_drum_assay_features_kernel(
                 nc.scalar.copy(dst, src)
             y_codes = held([P, HALF], I32, "y_codes%d" % h)
             nc.vector.quantize_mx(y_codes[:].bitcast(FP8X4), y_scales[:, cols], rounded[:])
-            nc.sync.dma_start(y_words[:, cols], y_codes[:])
+            (nc.scalar if last else nc.sync).dma_start(y_words[:, cols], y_codes[:])
         for q in range(4):
             queue = nc.scalar if q % 2 else nc.sync
             queue.dma_start(out_2[0, 4 * q : 4 * q + 4, :].bitcast(I32), y_scales[32 * q : 32 * q + 4, :].bitcast(I32))

@@ -87,44 +87,46 @@ def tile_list_drum_assay_features_kernel(
             return codes, scales
 
         offs2_t = load_list(offs2, "offs2_t")
-        tab2_win = load_words(tab2_words[0], "tab2_win", 34)
-        wb_raw = held([P, 2 * H], U8, "wb_raw")
-        nc.sync.dma_start(wb_raw[:].bitcast(I32), wb_words[0].bitcast(I32))
+        tab2_scale_win = load_scales(zeroed(placed([P, T], U8, "tab2_scale_win", 75), nc.gpsimd), tab2_scales, nc.sync)
+        warm = placed([P, 32], F32, "warm", 42 - 1 / 16)
+        nc.vector.memset(warm[:], 1.0)
+        tab3_scale_win = load_scales(zeroed(placed([P, T], U8, "tab3_scale_win", 12), nc.vector), tab3_scales, nc.sync)
+        tab_scale_win = load_scales(zeroed(placed([P, T], U8, "tab_scale_win", 59), nc.gpsimd), tab_scales, nc.gpsimd)
         offs3_t = load_list(offs3, "offs3_t")
         offs_t = load_list(offs, "offs_t")
         pos2_t = load_list(pos2, "pos2_t")
         pos1_t = load_list(pos1, "pos1_t")
         pos3_t = load_list(pos3, "pos3_t")
-        tab2_scale_win = load_scales(zeroed(placed([P, T], U8, "tab2_scale_win", 72), nc.gpsimd), tab2_scales, nc.gpsimd)
-        wb_scale_raw = load_scales(zeroed(placed([P, H], U8, "wb_scale_raw", 76), nc.vector), wb_scales, nc.sync)
-        tab3_scale_win = load_scales(zeroed(placed([P, T], U8, "tab3_scale_win", 67), nc.vector), tab3_scales, nc.sync)
-        wd_scale_raw = load_scales(zeroed(held([P, H], U8, "wd_scale_raw"), nc.vector), wd_scales, nc.sync)
-        warm = placed([P, 32], F32, "warm", 10 - 1 / 16)
-        nc.vector.memset(warm[:], 1.0)
+        wb_raw = placed([P, 2 * H], U8, "wb_raw", 9)
+        nc.sync.dma_start(wb_raw[:].bitcast(I32), wb_words[0].bitcast(I32))
         nc.scalar.activation(warm[:], warm[:], ACT.Sqrt)
+        tab2_win = load_words(tab2_words[0], "tab2_win", 42)
+        wb_scale_raw = load_scales(zeroed(placed([P, H], U8, "wb_scale_raw", 41), nc.vector), wb_scales, nc.sync)
 
-        v2_words = gather_words(tab2_win, offs2_t, held([P, S], U32, "v2_words"))
         wb_dealt = deal(wb_raw, held([P, 2 * H], U8, "wb_dealt"))
+        v2_scales = gather_scales(tab2_scale_win, offs2_t, held([P, S], U8, "v2_scales"))
+        v3_scales = gather_scales(tab3_scale_win, offs3_t, held([P, S], U8, "v3_scales"))
+        v2_words = [gather_words(tab2_win, offs2_t[:, 0:32], held([P, BANK], U32, "v2_words0"))]
         wb_scale_dealt = deal(wb_scale_raw, held([P, H], U8, "wb_scale_dealt"))
-        v2_scales = [
-            gather_scales(tab2_scale_win, offs2_t[:, 32 * h : 32 * h + 32], held([P, BANK], U8, "v2_scales%d" % h))
-            for h in range(2)
-        ]
+        v2_words.append(gather_words(tab2_win, offs2_t[:, 32:64], placed([P, BANK], U32, "v2_words1", 39.5)))
+
+        v_scales = gather_scales(tab_scale_win, offs_t, placed([P, S], U8, "v_scales", 41.5))
 
         tab3_win = load_words(tab3_words[0], "tab3_win", 10)
         wd_raw = placed([P, 4 * H], U8, "wd_raw", 6)
         nc.sync.dma_start(wd_raw[:].bitcast(I32), wd_words[0].rearrange("p n t -> p (n t)").bitcast(I32))
-        v3_scales = gather_scales(tab3_scale_win, offs3_t, placed([P, S], U8, "v3_scales", 75.5))
-        v3_words = gather_words(tab3_win, offs3_t, placed([P, S], U32, "v3_words", 68))
+        wd_scale_raw = load_scales(zeroed(placed([P, H], U8, "wd_scale_raw", 75), nc.gpsimd), wd_scales, nc.sync)
+        v3_words = gather_words(tab3_win, offs3_t, held([P, S], U32, "v3_words"))
         wd_dealt = deal(wd_raw, placed([P, 4 * H], U8, "wd_dealt", 19))
         wd_scale_dealt = deal(wd_scale_raw, placed([P, H], U8, "wd_scale_dealt", 18))
 
-        tab_win = [load_words(tab_words[a], "tab_win%d" % a, 36 + 16 * a) for a in range(2)]
-        tab_scale_win = load_scales(zeroed(placed([P, T], U8, "tab_scale_win", 31), nc.gpsimd), tab_scales, nc.sync)
-        v_scales = gather_scales(tab_scale_win, offs_t, held([P, S], U8, "v_scales"))
-        v_words = [gather_words(tab_win[a], offs_t, held([P, S], U32, "v_words%d" % a)) for a in range(2)]
+        tab_win = [load_words(tab_words[a], "tab_win%d" % a, 43 + 16 * a) for a in range(2)]
+        v_words = [
+            gather_words(tab_win[0], offs_t, placed([P, S], U32, "v_words0", 6)),
+            gather_words(tab_win[1], offs_t, held([P, S], U32, "v_words1")),
+        ]
 
-        wa_at = {(0, 0): 23, (0, 1): 10, (1, 0): 36, (1, 1): 44}
+        wa_at = {(0, 0): 23, (0, 1): 10, (1, 0): 43, (1, 1): 51}
         wa_raw = {}
         for (b, a), kib in wa_at.items():
             wa_raw[b, a] = placed([P, 4, BANK], F32, "wa_raw%d%d" % (b, a), kib)
@@ -154,7 +156,7 @@ def tile_list_drum_assay_features_kernel(
         def b_passes(s, h, cols):
             c = HALF * s[1] + P * s[0]
             return [(wb_dealt[:, 2 * c : 2 * c + 2 * P].bitcast(FP4X4), wb_scale_dealt[:, c : c + P],
-                     v2_words[:, cols].bitcast(FP8X4), v2_scales[h][:])]
+                     v2_words[h][:].bitcast(FP8X4), v2_scales[:, cols])]
 
         def d_passes(s, h, cols):
             c = HALF * s[1] + P * s[0]
@@ -173,13 +175,14 @@ def tile_list_drum_assay_features_kernel(
 
         wa_q = {}
 
-        def quantise_wa(b, a, copy):
+        def quantise_wa(b, a, copies):
             name = "wa%d%d" % (b, a)
             rounded = small([P, 4 * BANK], BF16, name + "_bf16")
-            copy(
-                rounded[:].rearrange("p (t g i j) -> p g t i j", t=4, i=8, j=4),
-                wa_raw[b, a][:].rearrange("p j (g t i) -> p g t i j", t=4, i=8),
-            )
+            share = 4 // len(copies)
+            src = wa_raw[b, a][:].rearrange("p j (g t i) -> p g t j i", t=4, i=8)
+            for n, copy in enumerate(copies):
+                dst = rounded[:, n * share * BANK : (n + 1) * share * BANK]
+                copy(dst.rearrange("p (t g i j) -> p g t j i", t=share, i=8, j=4), src[:, :, n * share : (n + 1) * share])
             wa_q[b, a] = quantise(rounded, name)
 
         def a_passes(s, h, cols):
@@ -205,39 +208,40 @@ def tile_list_drum_assay_features_kernel(
                 nc.scalar.activation(dst, src, ACT.Copy, scale=-1.0)
             return quantise(rounded, name)
 
-        pick_b(all_slices[0:4], 2)
-        pick_b(all_slices[4:6], 52)
-        quantise_wa(0, 0, nc.scalar.copy)
-        quantise_wa(0, 1, nc.scalar.copy)
+        pick_b(all_slices[0:2], 2)
+        pick_b(all_slices[2:4], 75)
+        pick_b(all_slices[4:6], 59)
+        quantise_wa(0, 0, [nc.vector.tensor_copy])
+        quantise_wa(0, 1, [nc.vector.tensor_copy, nc.scalar.copy])
         pick_b(all_slices[6:8], 10)
-        quantise_wa(1, 0, nc.scalar.copy)
-        wo_raw = [placed([P, 4, N], F32, "wo_raw%d" % b, kib) for b, kib in enumerate((23, 60))]
+        quantise_wa(1, 0, [nc.scalar.copy])
+        wo_raw = [placed([P, 4, N], F32, "wo_raw%d" % b, kib) for b, kib in enumerate((23, 67))]
         for b in range(2):
             rows = wo[BANK * b : BANK * (b + 1), :].rearrange("(g j i) n -> j g i n", j=4, i=8)
             for j in range(4):
                 nc.sync.dma_start(wo_raw[b][:, j, :], rows[j])
 
         a_sq0 = first_stage(all_slices[0:4], a_passes, ACT.Square, "sq")
-        neg_z0 = placed([P, 4, P2], F32, "neg_z0", 78)
+        neg_z0 = placed([P, 4, P2], F32, "neg_z0", 31)
         for t in range(4):
             if t == 1:
-                quantise_wa(1, 1, nc.scalar.copy)
+                quantise_wa(1, 1, [nc.scalar.copy])
             root((0, t), a_sq0, neg_z0[:, t, :])
             subtract((0, t), 0, P2, neg_z0[:, t, :])
         z0 = quantise_z(neg_z0, "z0", True)
 
         a_sq1 = first_stage(all_slices[4:8], a_passes, ACT.Square, "sq")
-        total1 = placed([P, 4, P2], F32, "total1", 36)
-        for t in range(4):
-            root((1, t), a_sq1, total1[:, t, :])
         wo_q = []
         for b in range(2):
-            rounded = placed([P, 4 * N], BF16, "wo%d_bf16" % b, 78 + 4 * b)
+            rounded = small([P, 4 * N], BF16, "wo%d_bf16" % b)
             nc.scalar.copy(
                 rounded[:].rearrange("p (t q j) -> p q j t", t=4, j=4),
                 wo_raw[b][:].rearrange("p j (q t) -> p q j t", t=4),
             )
             wo_q.append(quantise(rounded, "wo%d" % b))
+        total1 = placed([P, 4, P2], F32, "total1", 43)
+        for t in range(4):
+            root((1, t), a_sq1, total1[:, t, :])
 
         y_scales = held([P, P2], U8, "y_scales")
         y_rows = out_0.rearrange("(p t) m -> p t m", t=4)
@@ -254,7 +258,7 @@ def tile_list_drum_assay_features_kernel(
             last = h == 1
             cols = slice(HALF * h, HALF * (h + 1))
             accs = [psum.tile([P, HALF], F32, name="y_acc", tag="tail" if last else "acc", bufs=4) for t in range(4)]
-            neg_z1 = placed([P, 4, HALF], F32, "neg_z1_%d" % h, 44 + 4 * h)
+            neg_z1 = placed([P, 4, HALF], F32, "neg_z1_%d" % h, 51 - 8 * h)
             for t in range(4):
                 subtract((1, t), HALF * h, HALF, neg_z1[:, t, :])
             z1 = quantise_z(neg_z1, "z1_%d" % h, last)
@@ -262,7 +266,7 @@ def tile_list_drum_assay_features_kernel(
             for t in range(4):
                 project(accs[t], t, 0, z0, cols)
                 project(accs[t], t, 1, z1, slice(0, HALF))
-                if last and t % 2 == 1:
+                if last:
                     nc.vector.tensor_copy(y[:, t, :], accs[t][:])
                 else:
                     nc.scalar.copy(y[:, t, :], accs[t][:])

@@ -2,8 +2,8 @@ from contextlib import ExitStack
 
 import concourse.mybir as mybir
 
-K, K2, T, S, P2, H, N = 1024, 512, 4096, 1024, 512, 1024, 512
-FLOPS = 2 * H * S * (K + 2 * K2) + 2 * N * P2 * H
+K, M, T, S, J, H, N = 1024, 512, 4096, 1024, 512, 1024, 512
+FLOPS = 2 * H * S * (K + 2 * M) + 2 * N * J * H
 
 F32 = mybir.dt.float32
 BF16 = mybir.dt.bfloat16
@@ -17,8 +17,51 @@ ACT = mybir.ActivationFunctionType
 ALU = mybir.AluOpType
 
 P = 128
+PACK = 4
+PASS = P * PACK
+RUN = 8
 BANK = 512
-HALF = 256
+PER_COLUMN = 16
+HALF = J // 2
+SLICES = [(b, t) for b in range(H // PASS) for t in range(PACK)]
+
+AT = {
+    "b_picked00": 2,
+    "y0": 2,
+    "wd_raw": 6,
+    "v_words0": 6,
+    "y1": 6,
+    "wb_raw": 9,
+    "tab3_win": 10,
+    "wa_raw01": 10,
+    "b_picked12": 10,
+    "tab3_scale_win": 12,
+    "wd_scale_dealt": 18,
+    "wd_dealt": 19,
+    "wa_raw00": 23,
+    "wo_raw0": 23,
+    "neg_z0": 31,
+    "wo0_bf16": 31,
+    "wo1_bf16": 35,
+    "v2_words1": 39.5,
+    "wb_scale_raw": 41,
+    "v_scales": 41.5,
+    "warm": 41.9375,
+    "tab2_win": 42,
+    "tab_win0": 43,
+    "total1": 43,
+    "neg_z1_1": 43,
+    "wa_raw11": 51,
+    "neg_z1_0": 51,
+    "tab_scale_win": 59,
+    "tab_win1": 59,
+    "b_picked10": 59,
+    "wo_raw1": 67,
+    "b_picked02": 75.5,
+    "tab2_scale_win": 79,
+    "wd_scale_raw": 79,
+    "wa_raw10": 79.5,
+}
 
 
 def tile_list_drum_assay_features_kernel(
@@ -31,114 +74,117 @@ def tile_list_drum_assay_features_kernel(
         lists = ctx.enter_context(tc.tile_pool(name="lists", bufs=1))
         keep = ctx.enter_context(tc.tile_pool(name="keep", bufs=1))
         rings = ctx.enter_context(tc.tile_pool(name="rings", bufs=1))
-        arena = ctx.enter_context(tc.tile_pool(name="arena", bufs=1))
+        shared = ctx.enter_context(tc.tile_pool(name="shared", bufs=1))
         psum = ctx.enter_context(tc.psum_pool(name="psum", bufs=1))
 
         def held(shape, dtype, name):
             return keep.tile(shape, dtype, name=name, align_bytes=64)
 
-        def placed(shape, dtype, name, kib):
-            return arena.tile(shape, dtype, name=name, offset=int(1024 * kib), align_bytes=64)
+        def placed(shape, dtype, name):
+            return shared.tile(shape, dtype, name=name, offset=int(1024 * AT[name]), align_bytes=64)
 
-        def small(shape, dtype, name):
-            return rings.tile(shape, dtype, name=name, tag="small", bufs=4, align_bytes=64)
+        def rounded_tile(width, name):
+            return rings.tile([P, width], BF16, name=name, tag="rounded", bufs=4, align_bytes=64)
 
         def load_list(src, name):
             tile = lists.tile(list(src.shape), U16, name=name)
             nc.sync.dma_start(tile[:], src)
             return tile
 
-        def load_words(src, name, kib):
-            tile = placed([P, T], I32, name, kib)
+        def load_words(src, name):
+            tile = placed([P, src.shape[1]], I32, name)
             nc.sync.dma_start(tile[:], src.rearrange("p n t -> p (n t)").bitcast(I32))
             return tile
 
-        def load_scales(tile, src, queue):
+        def load_scales(src, name, zeroed_by, queue):
             passes = src.shape[0]
+            tile = placed([P, src.shape[2]], U8, name)
+            zeroed_by.memset(tile[:].bitcast(I32), 0)
             for q in range(4):
                 rows = src[0, 4 * q : 4 * q + 4, :] if passes == 1 else src[:, 4 * q : 4 * q + 4, :]
                 queue.dma_start(tile[32 * q : 32 * q + 4 * passes, :].bitcast(I32), rows.bitcast(I32))
-            return tile
-
-        def zeroed(tile, engine):
-            engine.memset(tile[:].bitcast(I32), 0)
             return tile
 
         def gather_words(window, offsets, picked):
             nc.vector.tensor_copy(picked[:], window[:].bitcast(U32).indirect(offsets[:]))
             return picked
 
-        def gather_scales(window, offsets, picked):
+        def gather(window, offsets, picked):
             nc.vector.tensor_copy(picked[:], window[:].indirect(offsets[:]))
             return picked
 
         def deal(raw, dealt):
             nc.vector.tensor_copy(
-                dealt[:].bitcast(I32).rearrange("p (t g i) -> p g t i", t=4, g=32),
-                raw[:].bitcast(I32).rearrange("p (g t i) -> p g t i", t=4, g=32),
+                dealt[:].bitcast(I32).rearrange("p (t g i) -> p g t i", t=PACK, g=H // 32),
+                raw[:].bitcast(I32).rearrange("p (g t i) -> p g t i", t=PACK, g=H // 32),
             )
             return dealt
 
         def quantise(rounded, name):
-            width = rounded.shape[1] // 4
+            width = rounded.shape[1] // PACK
             codes = held([P, width], U32, name + "_codes")
             scales = held([P, width], U8, name + "_scales")
             nc.vector.quantize_mx(codes[:].bitcast(FP8X4), scales[:], rounded[:])
             return codes, scales
 
+        def interleaved(rounded, planes):
+            return (
+                rounded[:].rearrange("p (c i t) -> p c t i", t=PACK, i=4),
+                planes[:].rearrange("p t (c i) -> p c t i", i=4),
+            )
+
         offs2_t = load_list(offs2, "offs2_t")
-        tab2_scale_win = load_scales(zeroed(placed([P, T], U8, "tab2_scale_win", 75), nc.gpsimd), tab2_scales, nc.sync)
-        warm = placed([P, 32], F32, "warm", 42 - 1 / 16)
+        tab2_scale_win = load_scales(tab2_scales, "tab2_scale_win", nc.gpsimd, nc.sync)
+        warm = placed([P, 32], F32, "warm")
         nc.vector.memset(warm[:], 1.0)
-        tab3_scale_win = load_scales(zeroed(placed([P, T], U8, "tab3_scale_win", 12), nc.vector), tab3_scales, nc.sync)
-        tab_scale_win = load_scales(zeroed(placed([P, T], U8, "tab_scale_win", 59), nc.gpsimd), tab_scales, nc.gpsimd)
+        tab3_scale_win = load_scales(tab3_scales, "tab3_scale_win", nc.vector, nc.sync)
+        tab_scale_win = load_scales(tab_scales, "tab_scale_win", nc.gpsimd, nc.gpsimd)
         offs3_t = load_list(offs3, "offs3_t")
         offs_t = load_list(offs, "offs_t")
         pos2_t = load_list(pos2, "pos2_t")
         pos1_t = load_list(pos1, "pos1_t")
         pos3_t = load_list(pos3, "pos3_t")
-        wb_raw = placed([P, 2 * H], U8, "wb_raw", 9)
+        wb_raw = placed([P, 2 * H], U8, "wb_raw")
         nc.sync.dma_start(wb_raw[:].bitcast(I32), wb_words[0].bitcast(I32))
         nc.scalar.activation(warm[:], warm[:], ACT.Sqrt)
-        tab2_win = load_words(tab2_words[0], "tab2_win", 42)
-        wb_scale_raw = load_scales(zeroed(placed([P, H], U8, "wb_scale_raw", 41), nc.vector), wb_scales, nc.sync)
+        tab2_win = load_words(tab2_words[0], "tab2_win")
+        wb_scale_raw = load_scales(wb_scales, "wb_scale_raw", nc.vector, nc.sync)
 
         wb_dealt = deal(wb_raw, held([P, 2 * H], U8, "wb_dealt"))
-        v2_scales = gather_scales(tab2_scale_win, offs2_t, held([P, S], U8, "v2_scales"))
-        v3_scales = gather_scales(tab3_scale_win, offs3_t, held([P, S], U8, "v3_scales"))
-        v2_words = [gather_words(tab2_win, offs2_t[:, 0:32], held([P, BANK], U32, "v2_words0"))]
+        v2_scales = gather(tab2_scale_win, offs2_t, held([P, S], U8, "v2_scales"))
+        v3_scales = gather(tab3_scale_win, offs3_t, held([P, S], U8, "v3_scales"))
+        bank_columns = BANK // PER_COLUMN
+        v2_words = [gather_words(tab2_win, offs2_t[:, :bank_columns], held([P, BANK], U32, "v2_words0"))]
         wb_scale_dealt = deal(wb_scale_raw, held([P, H], U8, "wb_scale_dealt"))
-        v2_words.append(gather_words(tab2_win, offs2_t[:, 32:64], placed([P, BANK], U32, "v2_words1", 39.5)))
+        v2_words.append(gather_words(tab2_win, offs2_t[:, bank_columns:], placed([P, BANK], U32, "v2_words1")))
+        v_scales = gather(tab_scale_win, offs_t, placed([P, S], U8, "v_scales"))
 
-        v_scales = gather_scales(tab_scale_win, offs_t, placed([P, S], U8, "v_scales", 41.5))
-
-        tab3_win = load_words(tab3_words[0], "tab3_win", 10)
-        wd_raw = placed([P, 4 * H], U8, "wd_raw", 6)
-        nc.sync.dma_start(wd_raw[:].bitcast(I32), wd_words[0].rearrange("p n t -> p (n t)").bitcast(I32))
-        wd_scale_raw = load_scales(zeroed(placed([P, H], U8, "wd_scale_raw", 75), nc.gpsimd), wd_scales, nc.sync)
+        tab3_win = load_words(tab3_words[0], "tab3_win")
+        wd_raw = load_words(wd_words[0], "wd_raw")
+        wd_scale_raw = load_scales(wd_scales, "wd_scale_raw", nc.vector, nc.sync)
         v3_words = gather_words(tab3_win, offs3_t, held([P, S], U32, "v3_words"))
-        wd_dealt = deal(wd_raw, placed([P, 4 * H], U8, "wd_dealt", 19))
-        wd_scale_dealt = deal(wd_scale_raw, placed([P, H], U8, "wd_scale_dealt", 18))
+        wd_dealt = deal(wd_raw, placed([P, H], I32, "wd_dealt"))
+        wd_scale_dealt = deal(wd_scale_raw, placed([P, H], U8, "wd_scale_dealt"))
 
-        tab_win = [load_words(tab_words[a], "tab_win%d" % a, 43 + 16 * a) for a in range(2)]
+        tab_win = [load_words(tab_words[a], "tab_win%d" % a) for a in range(K // PASS)]
         v_words = [
-            gather_words(tab_win[0], offs_t, placed([P, S], U32, "v_words0", 6)),
+            gather_words(tab_win[0], offs_t, placed([P, S], U32, "v_words0")),
             gather_words(tab_win[1], offs_t, held([P, S], U32, "v_words1")),
         ]
 
-        wa_at = {(0, 0): 23, (0, 1): 10, (1, 0): 43, (1, 1): 51}
         wa_raw = {}
-        for (b, a), kib in wa_at.items():
-            wa_raw[b, a] = placed([P, 4, BANK], F32, "wa_raw%d%d" % (b, a), kib)
-            rows = wa[BANK * a : BANK * (a + 1), BANK * b : BANK * (b + 1)]
-            nc.sync.dma_start(wa_raw[b, a][:], rows.rearrange("(p j) c -> p j c", j=4))
+        for b in range(H // PASS):
+            for a in range(K // PASS):
+                wa_raw[b, a] = placed([P, PACK, PASS], F32, "wa_raw%d%d" % (b, a))
+                rows = wa[PASS * a : PASS * (a + 1), PASS * b : PASS * (b + 1)]
+                nc.sync.dma_start(wa_raw[b, a][:], rows.rearrange("(p j) c -> p j c", j=PACK))
 
         def first_stage(slices, passes, func, tag):
             windows = {}
-            for pair in (slices[i : i + 2] for i in range(0, len(slices), 2)):
+            for pair in (slices[n : n + 2] for n in range(0, len(slices), 2)):
                 for s in pair:
-                    windows[s] = rings.tile([P, S], F32, name="%s%d%d" % (tag, s[0], s[1]), tag=tag, bufs=8)
-                for h in range(2):
+                    windows[s] = rings.tile([P, S], F32, name="%s%d%d" % (tag, s[0], s[1]), tag=tag, bufs=len(SLICES))
+                for h in range(S // BANK):
                     cols = slice(BANK * h, BANK * (h + 1))
                     for s in pair:
                         acc = psum.tile([P, BANK], F32, name="acc", tag="acc", bufs=4)
@@ -151,100 +197,101 @@ def tile_list_drum_assay_features_kernel(
                         nc.scalar.activation(windows[s][:, cols], acc[:], func)
             return windows
 
-        all_slices = [(b, t) for b in range(2) for t in range(4)]
+        def dealt_column(s):
+            return (H // PACK) * s[1] + P * s[0]
 
         def b_passes(s, h, cols):
-            c = HALF * s[1] + P * s[0]
+            c = dealt_column(s)
             return [(wb_dealt[:, 2 * c : 2 * c + 2 * P].bitcast(FP4X4), wb_scale_dealt[:, c : c + P],
                      v2_words[h][:].bitcast(FP8X4), v2_scales[:, cols])]
 
         def d_passes(s, h, cols):
-            c = HALF * s[1] + P * s[0]
-            return [(wd_dealt[:, 4 * c : 4 * c + 4 * P].bitcast(FP8X4), wd_scale_dealt[:, c : c + P],
+            c = dealt_column(s)
+            return [(wd_dealt[:, c : c + P].bitcast(FP8X4), wd_scale_dealt[:, c : c + P],
                      v3_words[:, cols].bitcast(FP8X4), v3_scales[:, cols])]
-
-        b_sq = first_stage(all_slices, b_passes, ACT.Square, "sq")
-        d_win = first_stage(all_slices, d_passes, ACT.Copy, "d")
-        b_picked = {}
-
-        def pick_b(slices, kib):
-            picked = placed([P, len(slices), P2], F32, "b_picked%d%d" % slices[0], kib)
-            for n, s in enumerate(slices):
-                b_picked[s] = picked[:, n, :]
-                nc.vector.tensor_copy(b_picked[s], b_sq[s][:].indirect(pos2_t[:]))
-
-        wa_q = {}
-
-        def quantise_wa(b, a, copies):
-            name = "wa%d%d" % (b, a)
-            rounded = small([P, 4 * BANK], BF16, name + "_bf16")
-            share = 4 // len(copies)
-            src = wa_raw[b, a][:].rearrange("p j (g t i) -> p g t j i", t=4, i=8)
-            for n, copy in enumerate(copies):
-                dst = rounded[:, n * share * BANK : (n + 1) * share * BANK]
-                copy(dst.rearrange("p (t g i j) -> p g t j i", t=share, i=8, j=4), src[:, :, n * share : (n + 1) * share])
-            wa_q[b, a] = quantise(rounded, name)
 
         def a_passes(s, h, cols):
             c = slice(P * s[1], P * (s[1] + 1))
             return [(wa_q[s[0], a][0][:, c].bitcast(FP8X4), wa_q[s[0], a][1][:, c],
-                     v_words[a][:, cols].bitcast(FP8X4), v_scales[4 * a : P, cols]) for a in range(2)]
+                     v_words[a][:, cols].bitcast(FP8X4), v_scales[4 * a : P, cols]) for a in range(K // PASS)]
+
+        b_picked = {}
+
+        def pick_b(pair):
+            picked = placed([P, len(pair), J], F32, "b_picked%d%d" % pair[0])
+            for n, s in enumerate(pair):
+                b_picked[s] = gather(b_sq[s], pos2_t, picked[:, n, :])
+
+        wa_q = {}
+
+        def quantise_wa(b, a, copy):
+            name = "wa%d%d" % (b, a)
+            rounded = rounded_tile(PACK * PASS, name + "_bf16")
+            copy(
+                rounded[:].rearrange("p (t g i j) -> p g t j i", t=PACK, i=RUN, j=PACK),
+                wa_raw[b, a][:].rearrange("p j (g t i) -> p g t j i", t=PACK, i=RUN),
+            )
+            wa_q[b, a] = quantise(rounded, name)
 
         def root(s, a_sq, total):
             nc.vector.tensor_tensor(total, a_sq[s][:].indirect(pos1_t[:]), b_picked[s], ALU.add)
             nc.scalar.activation(b_picked[s], total, ACT.Sqrt)
 
-        def subtract(s, first, count, neg_z):
-            picked_d = d_win[s][:].indirect(pos3_t[:, first // 16 : (first + count) // 16])
-            nc.vector.tensor_tensor(neg_z, picked_d, b_picked[s][:, first : first + count], ALU.subtract)
+        def subtract(s, cols, neg_z):
+            offsets = pos3_t[:, cols.start // PER_COLUMN : cols.stop // PER_COLUMN]
+            nc.vector.tensor_tensor(neg_z, d_win[s][:].indirect(offsets), b_picked[s][:, cols], ALU.subtract)
 
         def quantise_z(neg_z, name, on_vector):
-            rounded = small([P, 4 * neg_z.shape[2]], BF16, name + "_bf16")
-            dst = rounded[:].rearrange("p (c i t) -> p c t i", t=4, i=4)
-            src = neg_z[:].rearrange("p t (c i) -> p c t i", i=4)
+            rounded = rounded_tile(PACK * neg_z.shape[2], name + "_bf16")
+            dst, src = interleaved(rounded, neg_z)
             if on_vector:
                 nc.vector.tensor_scalar(dst, src, -1.0, None, ALU.mult)
             else:
                 nc.scalar.activation(dst, src, ACT.Copy, scale=-1.0)
             return quantise(rounded, name)
 
-        pick_b(all_slices[0:2], 2)
-        pick_b(all_slices[2:4], 75)
-        pick_b(all_slices[4:6], 59)
-        quantise_wa(0, 0, [nc.vector.tensor_copy])
-        quantise_wa(0, 1, [nc.vector.tensor_copy, nc.scalar.copy])
-        pick_b(all_slices[6:8], 10)
-        quantise_wa(1, 0, [nc.scalar.copy])
-        wo_raw = [placed([P, 4, N], F32, "wo_raw%d" % b, kib) for b, kib in enumerate((23, 67))]
-        for b in range(2):
-            rows = wo[BANK * b : BANK * (b + 1), :].rearrange("(g j i) n -> j g i n", j=4, i=8)
-            for j in range(4):
+        b_sq = first_stage(SLICES, b_passes, ACT.Square, "sq")
+        d_win = first_stage(SLICES, d_passes, ACT.Copy, "d")
+
+        pick_b(SLICES[0:2])
+        pick_b(SLICES[2:4])
+        pick_b(SLICES[4:6])
+        quantise_wa(0, 0, nc.vector.tensor_copy)
+        quantise_wa(0, 1, nc.scalar.copy)
+        pick_b(SLICES[6:8])
+        quantise_wa(1, 0, nc.scalar.copy)
+
+        wo_raw = [placed([P, PACK, N], F32, "wo_raw%d" % b) for b in range(H // PASS)]
+        for b in range(H // PASS):
+            rows = wo[PASS * b : PASS * (b + 1), :].rearrange("(g j i) n -> j g i n", j=PACK, i=RUN)
+            for j in range(PACK):
                 nc.sync.dma_start(wo_raw[b][:, j, :], rows[j])
 
-        a_sq0 = first_stage(all_slices[0:4], a_passes, ACT.Square, "sq")
-        neg_z0 = placed([P, 4, P2], F32, "neg_z0", 31)
-        for t in range(4):
-            if t == 1:
-                quantise_wa(1, 1, [nc.scalar.copy])
+        a_sq0 = first_stage(SLICES[:PACK], a_passes, ACT.Square, "sq")
+        neg_z0 = placed([P, PACK, J], F32, "neg_z0")
+        root((0, 0), a_sq0, neg_z0[:, 0, :])
+        subtract((0, 0), slice(0, J), neg_z0[:, 0, :])
+        quantise_wa(1, 1, nc.scalar.copy)
+        for t in range(1, PACK):
             root((0, t), a_sq0, neg_z0[:, t, :])
-            subtract((0, t), 0, P2, neg_z0[:, t, :])
-        z0 = quantise_z(neg_z0, "z0", True)
+            subtract((0, t), slice(0, J), neg_z0[:, t, :])
+        z0 = quantise_z(neg_z0, "z0", on_vector=True)
 
-        a_sq1 = first_stage(all_slices[4:8], a_passes, ACT.Square, "sq")
+        a_sq1 = first_stage(SLICES[PACK:], a_passes, ACT.Square, "sq")
         wo_q = []
-        for b in range(2):
-            rounded = small([P, 4 * N], BF16, "wo%d_bf16" % b)
+        for b in range(H // PASS):
+            rounded = placed([P, PACK * N], BF16, "wo%d_bf16" % b)
             nc.scalar.copy(
-                rounded[:].rearrange("p (t q j) -> p q j t", t=4, j=4),
-                wo_raw[b][:].rearrange("p j (q t) -> p q j t", t=4),
+                rounded[:].rearrange("p (t q j) -> p q j t", t=PACK, j=PACK),
+                wo_raw[b][:].rearrange("p j (q t) -> p q j t", t=PACK),
             )
             wo_q.append(quantise(rounded, "wo%d" % b))
-        total1 = placed([P, 4, P2], F32, "total1", 43)
-        for t in range(4):
+        total1 = placed([P, PACK, J], F32, "total1")
+        for t in range(PACK):
             root((1, t), a_sq1, total1[:, t, :])
 
-        y_scales = held([P, P2], U8, "y_scales")
-        y_rows = out_0.rearrange("(p t) m -> p t m", t=4)
+        y_scales = held([P, J], U8, "y_scales")
+        y_rows = out_0.rearrange("(p t) m -> p t m", t=PACK)
         y_words = out_1[0].rearrange("p m t -> p (m t)").bitcast(I32)
 
         def project(acc, t, b, z, cols):
@@ -254,30 +301,23 @@ def tile_list_drum_assay_features_kernel(
                 rhs=z[0][:, cols].bitcast(FP8X4), rhs_scale=z[1][:, cols], start=b == 0, stop=b == 1,
             )
 
-        for h in range(2):
-            last = h == 1
+        for h in range(J // HALF):
+            last = h == J // HALF - 1
+            copy = nc.vector.tensor_copy if last else nc.scalar.copy
             cols = slice(HALF * h, HALF * (h + 1))
-            accs = [psum.tile([P, HALF], F32, name="y_acc", tag="tail" if last else "acc", bufs=4) for t in range(4)]
-            neg_z1 = placed([P, 4, HALF], F32, "neg_z1_%d" % h, 51 - 8 * h)
-            for t in range(4):
-                subtract((1, t), HALF * h, HALF, neg_z1[:, t, :])
-            z1 = quantise_z(neg_z1, "z1_%d" % h, last)
-            y = placed([P, 4, HALF], F32, "y%d" % h, 2 + 4 * h)
-            for t in range(4):
+            accs = [psum.tile([P, HALF], F32, name="y_acc", tag="tail" if last else "acc", bufs=4) for t in range(PACK)]
+            neg_z1 = placed([P, PACK, HALF], F32, "neg_z1_%d" % h)
+            for t in range(PACK):
+                subtract((1, t), cols, neg_z1[:, t, :])
+            z1 = quantise_z(neg_z1, "z1_%d" % h, on_vector=last)
+            y = placed([P, PACK, HALF], F32, "y%d" % h)
+            for t in range(PACK):
                 project(accs[t], t, 0, z0, cols)
                 project(accs[t], t, 1, z1, slice(0, HALF))
-                if last:
-                    nc.vector.tensor_copy(y[:, t, :], accs[t][:])
-                else:
-                    nc.scalar.copy(y[:, t, :], accs[t][:])
+                copy(y[:, t, :], accs[t][:])
             nc.sync.dma_start(y_rows[:, :, cols], y[:])
-            rounded = small([P, 4 * HALF], BF16, "y%d_bf16" % h)
-            dst = rounded[:].rearrange("p (c i t) -> p c t i", t=4, i=4)
-            src = y[:].rearrange("p t (c i) -> p c t i", i=4)
-            if last:
-                nc.vector.tensor_copy(dst, src)
-            else:
-                nc.scalar.copy(dst, src)
+            rounded = rounded_tile(PACK * HALF, "y%d_bf16" % h)
+            copy(*interleaved(rounded, y))
             y_codes = held([P, HALF], I32, "y_codes%d" % h)
             nc.vector.quantize_mx(y_codes[:].bitcast(FP8X4), y_scales[:, cols], rounded[:])
             (nc.scalar if last else nc.sync).dma_start(y_words[:, cols], y_codes[:])

from contextlib import ExitStack

import concourse.mybir as mybir

K, M, T, S, J, H, N = 1024, 512, 4096, 1024, 512, 1024, 512
FLOPS = 2 * H * S * (K + 2 * M) + 2 * N * J * H

F32 = mybir.dt.float32
BF16 = mybir.dt.bfloat16
I32 = mybir.dt.int32
U32 = mybir.dt.uint32
U16 = mybir.dt.uint16
U8 = mybir.dt.uint8
FP8X4 = mybir.dt.float8_e4m3fn_x4
FP4X4 = mybir.dt.float4_e2m1fn_x4
ACT = mybir.ActivationFunctionType
ALU = mybir.AluOpType

P = 128
PACK = 4
PASS = P * PACK
RUN = 8
BANK = 512
PER_COLUMN = 16
HALF = J // 2
SLICES = [(b, t) for b in range(H // PASS) for t in range(PACK)]

AT = {
    "b_picked00": 2,
    "y0": 2,
    "wd_raw": 6,
    "v_words0": 6,
    "y1": 6,
    "wb_raw": 9,
    "tab3_win": 10,
    "wa_raw01": 10,
    "b_picked12": 10,
    "tab3_scale_win": 12,
    "wd_scale_dealt": 18,
    "wd_dealt": 19,
    "wa_raw00": 23,
    "wo_raw0": 23,
    "neg_z0": 31,
    "wo0_bf16": 31,
    "wo1_bf16": 35,
    "v2_words1": 39.5,
    "wb_scale_raw": 41,
    "v_scales": 41.5,
    "warm": 41.9375,
    "tab2_win": 42,
    "tab_win0": 43,
    "total1": 43,
    "neg_z1_1": 43,
    "wa_raw11": 51,
    "neg_z1_0": 51,
    "tab_scale_win": 59,
    "tab_win1": 59,
    "b_picked10": 59,
    "wo_raw1": 67,
    "b_picked02": 75.5,
    "tab2_scale_win": 79,
    "wd_scale_raw": 79,
    "wa_raw10": 79.5,
}


def tile_list_drum_assay_features_kernel(
    tc, tab_words, tab_scales, tab2_words, tab2_scales, tab3_words, tab3_scales,
    offs, offs2, offs3, pos1, pos2, pos3, wa, wb_words, wb_scales, wd_words, wd_scales, wo,
    out_0, out_1, out_2,
):
    nc = tc.nc
    with ExitStack() as ctx:
        lists = ctx.enter_context(tc.tile_pool(name="lists", bufs=1))
        keep = ctx.enter_context(tc.tile_pool(name="keep", bufs=1))
        rings = ctx.enter_context(tc.tile_pool(name="rings", bufs=1))
        shared = ctx.enter_context(tc.tile_pool(name="shared", bufs=1))
        psum = ctx.enter_context(tc.psum_pool(name="psum", bufs=1))

        def held(shape, dtype, name):
            return keep.tile(shape, dtype, name=name, align_bytes=64)

        def placed(shape, dtype, name):
            return shared.tile(shape, dtype, name=name, offset=int(1024 * AT[name]), align_bytes=64)

        def rounded_tile(width, name):
            return rings.tile([P, width], BF16, name=name, tag="rounded", bufs=4, align_bytes=64)

        def load_list(src, name):
            tile = lists.tile(list(src.shape), U16, name=name)
            nc.sync.dma_start(tile[:], src)
            return tile

        def load_words(src, name):
            tile = placed([P, src.shape[1]], I32, name)
            nc.sync.dma_start(tile[:], src.rearrange("p n t -> p (n t)").bitcast(I32))
            return tile

        def load_scales(src, name, zeroed_by, queue):
            passes = src.shape[0]
            tile = placed([P, src.shape[2]], U8, name)
            zeroed_by.memset(tile[:].bitcast(I32), 0)
            for q in range(4):
                rows = src[0, 4 * q : 4 * q + 4, :] if passes == 1 else src[:, 4 * q : 4 * q + 4, :]
                queue.dma_start(tile[32 * q : 32 * q + 4 * passes, :].bitcast(I32), rows.bitcast(I32))
            return tile

        def gather_words(window, offsets, picked):
            nc.vector.tensor_copy(picked[:], window[:].bitcast(U32).indirect(offsets[:]))
            return picked

        def gather(window, offsets, picked):
            nc.vector.tensor_copy(picked[:], window[:].indirect(offsets[:]))
            return picked

        def deal(raw, dealt):
            nc.vector.tensor_copy(
                dealt[:].bitcast(I32).rearrange("p (t g i) -> p g t i", t=PACK, g=H // 32),
                raw[:].bitcast(I32).rearrange("p (g t i) -> p g t i", t=PACK, g=H // 32),
            )
            return dealt

        def quantise(rounded, name):
            width = rounded.shape[1] // PACK
            codes = held([P, width], U32, name + "_codes")
            scales = held([P, width], U8, name + "_scales")
            nc.vector.quantize_mx(codes[:].bitcast(FP8X4), scales[:], rounded[:])
            return codes, scales

        def interleaved(rounded, planes):
            return (
                rounded[:].rearrange("p (c i t) -> p c t i", t=PACK, i=4),
                planes[:].rearrange("p t (c i) -> p c t i", i=4),
            )

        offs2_t = load_list(offs2, "offs2_t")
        tab2_scale_win = load_scales(tab2_scales, "tab2_scale_win", nc.gpsimd, nc.sync)
        warm = placed([P, 32], F32, "warm")
        nc.vector.memset(warm[:], 1.0)
        tab3_scale_win = load_scales(tab3_scales, "tab3_scale_win", nc.vector, nc.sync)
        tab_scale_win = load_scales(tab_scales, "tab_scale_win", nc.gpsimd, nc.gpsimd)
        offs3_t = load_list(offs3, "offs3_t")
        offs_t = load_list(offs, "offs_t")
        pos2_t = load_list(pos2, "pos2_t")
        pos1_t = load_list(pos1, "pos1_t")
        pos3_t = load_list(pos3, "pos3_t")
        wb_raw = placed([P, 2 * H], U8, "wb_raw")
        nc.sync.dma_start(wb_raw[:].bitcast(I32), wb_words[0].bitcast(I32))
        nc.scalar.activation(warm[:], warm[:], ACT.Sqrt)
        tab2_win = load_words(tab2_words[0], "tab2_win")
        wb_scale_raw = load_scales(wb_scales, "wb_scale_raw", nc.vector, nc.sync)

        wb_dealt = deal(wb_raw, held([P, 2 * H], U8, "wb_dealt"))
        v2_scales = gather(tab2_scale_win, offs2_t, held([P, S], U8, "v2_scales"))
        v3_scales = gather(tab3_scale_win, offs3_t, held([P, S], U8, "v3_scales"))
        bank_columns = BANK // PER_COLUMN
        v2_words = [gather_words(tab2_win, offs2_t[:, :bank_columns], held([P, BANK], U32, "v2_words0"))]
        wb_scale_dealt = deal(wb_scale_raw, held([P, H], U8, "wb_scale_dealt"))
        v2_words.append(gather_words(tab2_win, offs2_t[:, bank_columns:], placed([P, BANK], U32, "v2_words1")))
        v_scales = gather(tab_scale_win, offs_t, placed([P, S], U8, "v_scales"))

        tab3_win = load_words(tab3_words[0], "tab3_win")
        wd_raw = load_words(wd_words[0], "wd_raw")
        wd_scale_raw = load_scales(wd_scales, "wd_scale_raw", nc.vector, nc.sync)
        v3_words = gather_words(tab3_win, offs3_t, held([P, S], U32, "v3_words"))
        wd_dealt = deal(wd_raw, placed([P, H], I32, "wd_dealt"))
        wd_scale_dealt = deal(wd_scale_raw, placed([P, H], U8, "wd_scale_dealt"))

        tab_win = [load_words(tab_words[a], "tab_win%d" % a) for a in range(K // PASS)]
        v_words = [
            gather_words(tab_win[0], offs_t, placed([P, S], U32, "v_words0")),
            gather_words(tab_win[1], offs_t, held([P, S], U32, "v_words1")),
        ]

        wa_raw = {}
        for b in range(H // PASS):
            for a in range(K // PASS):
                wa_raw[b, a] = placed([P, PACK, PASS], F32, "wa_raw%d%d" % (b, a))
                rows = wa[PASS * a : PASS * (a + 1), PASS * b : PASS * (b + 1)]
                nc.sync.dma_start(wa_raw[b, a][:], rows.rearrange("(p j) c -> p j c", j=PACK))

        def first_stage(slices, passes, func, tag):
            windows = {}
            for pair in (slices[n : n + 2] for n in range(0, len(slices), 2)):
                for s in pair:
                    windows[s] = rings.tile([P, S], F32, name="%s%d%d" % (tag, s[0], s[1]), tag=tag, bufs=len(SLICES))
                for h in range(S // BANK):
                    cols = slice(BANK * h, BANK * (h + 1))
                    for s in pair:
                        acc = psum.tile([P, BANK], F32, name="acc", tag="acc", bufs=4)
                        operands = passes(s, h, cols)
                        for n, (w, w_scale, v, v_scale) in enumerate(operands):
                            nc.tensor.matmul_mx(
                                acc[:], lhsT=w, lhsT_scale=w_scale, rhs=v, rhs_scale=v_scale,
                                start=n == 0, stop=n == len(operands) - 1,
                            )
                        nc.scalar.activation(windows[s][:, cols], acc[:], func)
            return windows

        def dealt_column(s):
            return (H // PACK) * s[1] + P * s[0]

        def b_passes(s, h, cols):
            c = dealt_column(s)
            return [(wb_dealt[:, 2 * c : 2 * c + 2 * P].bitcast(FP4X4), wb_scale_dealt[:, c : c + P],
                     v2_words[h][:].bitcast(FP8X4), v2_scales[:, cols])]

        def d_passes(s, h, cols):
            c = dealt_column(s)
            return [(wd_dealt[:, c : c + P].bitcast(FP8X4), wd_scale_dealt[:, c : c + P],
                     v3_words[:, cols].bitcast(FP8X4), v3_scales[:, cols])]

        def a_passes(s, h, cols):
            c = slice(P * s[1], P * (s[1] + 1))
            return [(wa_q[s[0], a][0][:, c].bitcast(FP8X4), wa_q[s[0], a][1][:, c],
                     v_words[a][:, cols].bitcast(FP8X4), v_scales[4 * a : P, cols]) for a in range(K // PASS)]

        b_picked = {}

        def pick_b(pair):
            picked = placed([P, len(pair), J], F32, "b_picked%d%d" % pair[0])
            for n, s in enumerate(pair):
                b_picked[s] = gather(b_sq[s], pos2_t, picked[:, n, :])

        wa_q = {}

        def quantise_wa(b, a, copy):
            name = "wa%d%d" % (b, a)
            rounded = rounded_tile(PACK * PASS, name + "_bf16")
            copy(
                rounded[:].rearrange("p (t g i j) -> p g t j i", t=PACK, i=RUN, j=PACK),
                wa_raw[b, a][:].rearrange("p j (g t i) -> p g t j i", t=PACK, i=RUN),
            )
            wa_q[b, a] = quantise(rounded, name)

        def root(s, a_sq, total):
            nc.vector.tensor_tensor(total, a_sq[s][:].indirect(pos1_t[:]), b_picked[s], ALU.add)
            nc.scalar.activation(b_picked[s], total, ACT.Sqrt)

        def subtract(s, cols, neg_z):
            offsets = pos3_t[:, cols.start // PER_COLUMN : cols.stop // PER_COLUMN]
            nc.vector.tensor_tensor(neg_z, d_win[s][:].indirect(offsets), b_picked[s][:, cols], ALU.subtract)

        def quantise_z(neg_z, name, on_vector):
            rounded = rounded_tile(PACK * neg_z.shape[2], name + "_bf16")
            dst, src = interleaved(rounded, neg_z)
            if on_vector:
                nc.vector.tensor_scalar(dst, src, -1.0, None, ALU.mult)
            else:
                nc.scalar.activation(dst, src, ACT.Copy, scale=-1.0)
            return quantise(rounded, name)

        b_sq = first_stage(SLICES, b_passes, ACT.Square, "sq")
        d_win = first_stage(SLICES, d_passes, ACT.Copy, "d")

        pick_b(SLICES[0:2])
        pick_b(SLICES[2:4])
        pick_b(SLICES[4:6])
        quantise_wa(0, 0, nc.vector.tensor_copy)
        quantise_wa(0, 1, nc.scalar.copy)
        pick_b(SLICES[6:8])
        quantise_wa(1, 0, nc.scalar.copy)

        wo_raw = [placed([P, PACK, N], F32, "wo_raw%d" % b) for b in range(H // PASS)]
        for b in range(H // PASS):
            rows = wo[PASS * b : PASS * (b + 1), :].rearrange("(g j i) n -> j g i n", j=PACK, i=RUN)
            for j in range(PACK):
                nc.sync.dma_start(wo_raw[b][:, j, :], rows[j])

        a_sq0 = first_stage(SLICES[:PACK], a_passes, ACT.Square, "sq")
        neg_z0 = placed([P, PACK, J], F32, "neg_z0")
        root((0, 0), a_sq0, neg_z0[:, 0, :])
        subtract((0, 0), slice(0, J), neg_z0[:, 0, :])
        quantise_wa(1, 1, nc.scalar.copy)
        for t in range(1, PACK):
            root((0, t), a_sq0, neg_z0[:, t, :])
            subtract((0, t), slice(0, J), neg_z0[:, t, :])
        z0 = quantise_z(neg_z0, "z0", on_vector=True)

        a_sq1 = first_stage(SLICES[PACK:], a_passes, ACT.Square, "sq")
        wo_q = []
        for b in range(H // PASS):
            rounded = placed([P, PACK * N], BF16, "wo%d_bf16" % b)
            nc.scalar.copy(
                rounded[:].rearrange("p (t q j) -> p q j t", t=PACK, j=PACK),
                wo_raw[b][:].rearrange("p j (q t) -> p q j t", t=PACK),
            )
            wo_q.append(quantise(rounded, "wo%d" % b))
        total1 = placed([P, PACK, J], F32, "total1")
        for t in range(PACK):
            root((1, t), a_sq1, total1[:, t, :])

        y_scales = held([P, J], U8, "y_scales")
        y_rows = out_0.rearrange("(p t) m -> p t m", t=PACK)
        y_words = out_1[0].rearrange("p m t -> p (m t)").bitcast(I32)

        def project(acc, t, b, z, cols):
            c = slice(P * t, P * (t + 1))
            nc.tensor.matmul_mx(
                acc[:], lhsT=wo_q[b][0][:, c].bitcast(FP8X4), lhsT_scale=wo_q[b][1][:, c],
                rhs=z[0][:, cols].bitcast(FP8X4), rhs_scale=z[1][:, cols], start=b == 0, stop=b == 1,
            )

        for h in range(J // HALF):
            last = h == J // HALF - 1
            copy = nc.vector.tensor_copy if last else nc.scalar.copy
            cols = slice(HALF * h, HALF * (h + 1))
            accs = [psum.tile([P, HALF], F32, name="y_acc", tag="tail" if last else "acc", bufs=4) for t in range(PACK)]
            neg_z1 = placed([P, PACK, HALF], F32, "neg_z1_%d" % h)
            for t in range(PACK):
                subtract((1, t), cols, neg_z1[:, t, :])
            z1 = quantise_z(neg_z1, "z1_%d" % h, on_vector=last)
            y = placed([P, PACK, HALF], F32, "y%d" % h)
            for t in range(PACK):
                project(accs[t], t, 0, z0, cols)
                project(accs[t], t, 1, z1, slice(0, HALF))
                copy(y[:, t, :], accs[t][:])
            nc.sync.dma_start(y_rows[:, :, cols], y[:])
            rounded = rounded_tile(PACK * HALF, "y%d_bf16" % h)
            copy(*interleaved(rounded, y))
            y_codes = held([P, HALF], I32, "y_codes%d" % h)
            nc.vector.quantize_mx(y_codes[:].bitcast(FP8X4), y_scales[:, cols], rounded[:])
            (nc.scalar if last else nc.sync).dma_start(y_words[:, cols], y_codes[:])
        for q in range(4):
            queue = nc.scalar if q % 2 else nc.sync
            queue.dma_start(out_2[0, 4 * q : 4 * q + 4, :].bitcast(I32), y_scales[32 * q : 32 * q + 4, :].bitcast(I32))
